import numpy as np
import ml_dtypes


def mxq(x, axis, fmt="e4m3"):
    dtype, down = {"e4m3": (ml_dtypes.float8_e4m3fn, 7), "e5m2": (ml_dtypes.float8_e5m2, 14)}[fmt]
    v = np.moveaxis(np.asarray(x, np.float32).astype(ml_dtypes.bfloat16).astype(np.float64), axis, -1)
    blocks = v.reshape(v.shape[:-1] + (-1, 32))
    amax = np.abs(blocks).max(-1, keepdims=True)
    byte = np.maximum(np.where(amax > 0, np.frexp(amax)[1] - 1 + 127, 0) - down, 1)
    scale = np.exp2(byte - 127.0)
    codes = (blocks / scale).astype(np.float32).astype(dtype).astype(np.float64)
    return np.moveaxis((codes * scale).reshape(v.shape), -1, axis)


WIDE = False


def mx_kscale(k):
    if not WIDE:
        return np.ones(k)
    levels = np.array([10, -10, 5, -5, 0])
    if k % 512:
        return np.exp2(np.random.permutation(np.resize(levels, k // 32))).repeat(32)
    a = np.empty((k // 512, 16))
    for p in range(k // 512):
        a[p, :8] = np.random.permutation(np.resize(levels, 8))
        for g in range(8):
            far = levels[np.abs(levels - a[p, g]) >= 10]
            a[p, g + 8] = far[np.random.randint(len(far))]
    return np.exp2(a.ravel()).repeat(32)


def f64(x):
    return np.asarray(x).astype(np.float64)


def striped(idx):
    return np.tile(idx.reshape(-1, 16).T, (8, 1)).astype(np.uint16)


def unstriped(offs):
    return offs[:16].T.reshape(-1).astype(np.int64)


E2M1 = np.array([0.0, 0.5, 1.0, 1.5, 2.0, 3.0, 4.0, 6.0, -0.0, -0.5, -1.0, -1.5, -2.0, -3.0, -4.0, -6.0])


def pack_weight(w, fmt):
    k, n = w.shape
    w = f64(np.asarray(w, np.float32).astype(ml_dtypes.bfloat16)).reshape(k // 32, 32, n)
    amax = np.abs(w).max(1)
    if fmt == "e4m3":
        byte = np.frexp(amax)[1] - 1 + 127 - 7
    else:
        mant, ex = np.frexp(amax / 6.0)
        byte = np.where(mant > 0.5, ex, ex - 1) + 127
    byte = np.clip(np.where(amax > 0, byte, 1), 1, 254)
    scaled = (w * np.exp2(127.0 - byte)[:, None, :]).reshape(k, n).astype(np.float32)
    by_word = np.ascontiguousarray(scaled.reshape(k // 512, 128, 4, n).transpose(0, 1, 3, 2))
    if fmt == "e4m3":
        words = by_word.astype(ml_dtypes.float8_e4m3fn).view(np.uint8)
    else:
        c = by_word.astype(ml_dtypes.float4_e2m1fn).view(np.uint8) & 0xF
        words = (c[..., 0::2] | (c[..., 1::2] << 4)).reshape(k // 512, 128, 2 * n)
    return np.ascontiguousarray(words), np.ascontiguousarray(byte.astype(np.uint8).reshape(k // 512, 16, n))


def unpack_weight(words, scales, fmt):
    g, _, n = scales.shape
    words = np.ascontiguousarray(words).reshape(g, 128, n, -1)
    if fmt == "e4m3":
        vals = words.view(ml_dtypes.float8_e4m3fn).astype(np.float64)
    else:
        nib = np.empty((g, 128, n, 4), np.uint8)
        nib[..., 0::2] = words & 0xF
        nib[..., 1::2] = words >> 4
        vals = E2M1[nib]
    vals = vals * np.repeat(np.exp2(scales.astype(np.float64) - 127.0), 8, axis=1)[..., None]
    return vals.transpose(0, 1, 3, 2).reshape(g * 512, n)


def gelu(v):
    return 0.5 * v * (1.0 + np.tanh(np.sqrt(2.0 / np.pi) * (v + 0.044715 * v**3)))


def striped8(idx):
    return np.concatenate([v.reshape(-1, 16).T for v in idx]).astype(np.uint16)


def unstriped8(offs):
    return np.stack([offs[16 * g:16 * g + 16].T.reshape(-1) for g in range(8)]).astype(np.int64)


def heads(h, wgt, idx8):
    r = np.arange(h.shape[0])
    return wgt[r // 4 % 128] * h[r[:, None], idx8[r % 512 // 64]]


T, S, K, K1, K2, H, N, T2, P = 4096, 1024, 1536, 1024, 512, 1024, 512, 2048, 1024


def setup_inputs():
    n = np.random.standard_normal
    s = mx_kscale(K)[:, None]
    u = mx_kscale(H)[:, None]
    tab_words, tab_scales = pack_weight(n((K, T)) * s, "e4m3")
    w2_words, w2_scales = pack_weight(n((K2, H)) / np.sqrt(K2) / s[K1:], "e2m1")
    return {
        "tab_words": tab_words, "tab_scales": tab_scales,
        "offs": striped(np.random.permutation(T)[:S]),
        "w1": (n((K1, H)) / np.sqrt(K1) / s[:K1]).astype(np.float32),
        "w2_words": w2_words, "w2_scales": w2_scales,
        "b1": (0.6 * n(H)).astype(np.float32),
        "gain": (np.random.uniform(0.8, 1.8, H) * u[:, 0]).astype(np.float32),
        "wgs": np.exp(0.3 * n((128, S))).astype(np.float32),
        "page0": (n((H, T2)) * u).astype(np.float32),
        "offs2": striped(np.random.permutation(T2)[:S]),
        "wgt": np.repeat(np.random.uniform(0.5, 2.0, (8, P)), 16, axis=0).astype(np.float32),
        "offs3": striped8(np.stack([np.random.permutation(T2)[:P] for _ in range(8)])),
        "vis": np.random.uniform(0.2, 1.8, (H, P)).astype(np.float32),
        "w3": (n((H, N)) / np.sqrt(H) / u).astype(np.float32),
    }


def reference(tab_words, tab_scales, offs, w1, w2_words, w2_scales, b1, gain, wgs, page0, offs2, wgt, offs3, vis, w3):
    v = unpack_weight(tab_words, tab_scales, "e4m3")[:, unstriped(offs)]
    wc = mxq(f64(w1), 0, "e4m3")
    wi = unpack_weight(w2_words, w2_scales, "e2m1")
    d = wc.T @ v[:K1] + wi.T @ v[K1:]
    h = f64(gain)[:, None] * np.tanh(d + f64(b1)[:, None])
    page = f64(page0).copy()
    page[:, unstriped(offs2)] = np.tile(f64(wgs), (H // 128, 1)) * h
    x = heads(page, f64(wgt), unstriped8(offs3))
    z = mxq(x * f64(vis), 0, "e4m3")
    out = mxq(f64(w3), 0, "e4m3").T @ z
    return out

@@ -1,0 +1,355 @@
+from contextlib import ExitStack
+
+import concourse.mybir as mybir
+
+F32 = mybir.dt.float32
+BF16 = mybir.dt.bfloat16
+I32 = mybir.dt.int32
+U32 = mybir.dt.uint32
+U16 = mybir.dt.uint16
+U8 = mybir.dt.uint8
+FP8X4 = mybir.dt.float8_e4m3fn_x4
+FP4X4 = mybir.dt.float4_e2m1fn_x4
+MULT = mybir.AluOpType.mult
+COPY = mybir.ActivationFunctionType.Copy
+TANH = mybir.ActivationFunctionType.Tanh
+
+T, S, H, N, T2, M = 4096, 1024, 1024, 512, 2048, 1024
+P = 128
+FLOPS = 2 * 1536 * H * S + 2 * H * N * M
+SCALE_ROW = (4, 8, 0)
+TAIL = (256, 256, 256, 128, 128)
+
+
+def tile_list_drone_gate_features_kernel(
+    tc, tab_words, tab_scales, offs, w1, w2_words, w2_scales, b1, gain, wgs, page0, offs2, wgt, offs3, vis, w3, out
+):
+    nc = tc.nc
+    with ExitStack() as ctx:
+        lists = ctx.enter_context(tc.tile_pool(name="lists", bufs=1))
+        keep = ctx.enter_context(tc.tile_pool(name="keep", bufs=1))
+        ring = ctx.enter_context(tc.tile_pool(name="ring", bufs=1))
+        psum = ctx.enter_context(tc.psum_pool(name="psum", bufs=1))
+
+        idx = lists.tile([P, S // 16], U16, name="idx")
+        idx2 = lists.tile([P, S // 16], U16, name="idx2")
+        idx3 = lists.tile([P, M // 16], U16, name="idx3")
+
+        def big(name, tag, dtype):
+            return keep.tile([P, 4096], dtype, name=name, tag=tag, align_bytes=64)
+
+        def bank(k, name):
+            return psum.tile([P, 512], F32, name=name, tag="bank%d" % k)
+
+        tsc = keep.tile([P, T], U8, name="tsc", tag="tsc", align_bytes=64)
+        w2s_raw = keep.tile([P, H], U8, name="w2s_raw", align_bytes=64)
+        nc.vector.memset(w2s_raw[:].bitcast(I32), 0)
+        nc.vector.memset(tsc[:].bitcast(I32), 0)
+        ts32 = tab_scales.bitcast(I32)
+        w2s32 = w2_scales.bitcast(I32)
+        for q in range(4):
+            nc.gpsimd.dma_start(out=w2s_raw[32 * q : 32 * q + 4, :].bitcast(I32), in_=w2s32[0, 4 * q : 4 * q + 4, :])
+        for q in range(4):
+            nc.gpsimd.dma_start(out=tsc[32 * q + 4 : 32 * q + 12, :].bitcast(I32), in_=ts32[0:2, 4 * q : 4 * q + 4, :])
+            nc.gpsimd.dma_start(out=tsc[32 * q : 32 * q + 4, :].bitcast(I32), in_=ts32[2, 4 * q : 4 * q + 4, :])
+        b1_sb = keep.tile([P, 2, 4], F32, name="b1_sb")
+        gain_sb = keep.tile([P, 2, 4], F32, name="gain_sb")
+
+        def load_w(name, rows):
+            raw = ring.tile([P, 4, 512], F32, name=name, tag="wraw", bufs=2)
+            nc.sync.dma_start(out=raw[:], in_=rows.rearrange("(p j) c -> p j c", j=4))
+            return raw
+
+        def grouped_tile(name):
+            return ring.tile([P, 2048], BF16, name=name, tag="grouped", bufs=3, align_bytes=64)
+
+        def quantise(name, grouped, width):
+            codes = keep.tile([P, width], U32, name=name + "_codes", align_bytes=64)
+            scales = keep.tile([P, width], U8, name=name + "_scales", align_bytes=64)
+            nc.vector.quantize_mx(out=codes[:].bitcast(FP8X4), scales=scales[:], in_=grouped[:, : 4 * width])
+            return codes, scales
+
+        def group_w1(g, raw):
+            nc.scalar.copy(
+                out=g[:, :].rearrange("p (t m j) -> p m j t", t=4, j=4), in_=raw[:].rearrange("p j (m t) -> p m j t", t=4)
+            )
+            return g
+
+        def weave(engine_copy, g, planes, width):
+            engine_copy(
+                out=g[:, : 4 * width].rearrange("p (c k j) -> p c j k", k=4, j=4),
+                in_=planes.rearrange("p j (c k) -> p c j k", k=4),
+            )
+            return g
+
+        wgs_rows = wgs.rearrange("(q i) j -> q i j", i=4)
+        wgs_sb = [keep.tile([P, n, S], F32, name="wgs%d" % k) for k, n in enumerate((1, 1, 2))]
+
+        def load_wgs(k, i0, i1):
+            for a in (0, 2, 1, 3):
+                nc.sync.dma_start(out=wgs_sb[k][32 * a : 32 * a + 32, :, :], in_=wgs_rows[:, i0:i1, :])
+
+        wgs_of = [wgs_sb[0][:, 0, :], wgs_sb[1][:, 0, :], wgs_sb[2][:, 0, :], wgs_sb[2][:, 1, :]]
+
+        page_rows = page0.rearrange("(b p i) t -> b i p t", b=2, i=4)
+        vis_rows = vis.rearrange("(b p i) m -> b i p m", b=2, i=4)
+
+        def load_page(k):
+            t = ring.tile([P, T2], F32, name="page%d" % k, tag="page", bufs=5)
+            nc.sync.dma_start(out=t[:], in_=page_rows[k // 4, k % 4])
+            return t
+
+        def load_vis(k):
+            t = ring.tile([P, M], F32, name="vis%d" % k, tag="vis", bufs=4)
+            nc.sync.dma_start(out=t[:], in_=vis_rows[k // 4, k % 4])
+            return t
+
+        w1_raw = {}
+        for a in range(2):
+            w1_raw[a, 0] = load_w("w1raw%d0" % a, w1[512 * a : 512 * a + 512, 0:512])
+        load_wgs(0, 0, 1)
+        w2_raw = keep.tile([P, 2 * H], U8, name="w2_raw", align_bytes=64)
+        nc.sync.dma_start(out=w2_raw[:].bitcast(I32), in_=w2_words[0].bitcast(I32))
+        nc.sync.dma_start(idx[:], offs)
+        tab = []
+        for a in range(3):
+            t = big("tab%d" % a, "big%d" % a, I32)
+            nc.sync.dma_start(out=t[:], in_=tab_words[a].rearrange("p t i -> p (t i)").bitcast(I32))
+            tab.append(t)
+            if a == 0:
+                nc.sync.dma_start(out=gain_sb[:], in_=gain.rearrange("(b p i) -> p b i", b=2, i=4))
+        nc.sync.dma_start(out=b1_sb[:], in_=b1.rearrange("(b p i) -> p b i", b=2, i=4))
+        nc.sync.dma_start(idx2[:], offs2)
+        nc.sync.dma_start(idx3[:], offs3)
+        page = {0: load_page(0)}
+        load_wgs(1, 1, 2)
+        page[1] = load_page(1)
+        wgt_sb = keep.tile([P, M], F32, name="wgt_sb")
+        nc.sync.dma_start(out=wgt_sb[:], in_=wgt)
+        visb = {0: load_vis(0)}
+        load_wgs(2, 2, 4)
+        page[2] = load_page(2)
+        for a in range(2):
+            w1_raw[a, 1] = load_w("w1raw%d1" % a, w1[512 * a : 512 * a + 512, 512:1024])
+        visb[1] = load_vis(1)
+        page[3] = load_page(3)
+        visb[2] = load_vis(2)
+        visb[3] = load_vis(3)
+        page[4] = load_page(4)
+
+        w2c = keep.tile([P, 2 * H], U8, name="w2c", align_bytes=64)
+        w2s = keep.tile([P, H], U8, name="w2s", align_bytes=64)
+        nc.vector.tensor_copy(
+            out=w2c[:].rearrange("p (b i q e) -> p b i q e", b=2, i=4, e=2),
+            in_=w2_raw[:].rearrange("p (b q i e) -> p b i q e", b=2, i=4, e=2),
+        )
+        w1q = {}
+        for a in range(2):
+            w1q[a, 0] = quantise("w1q%d0" % a, group_w1(grouped_tile("g_w1_%d0" % a), w1_raw[a, 0]), 512)
+        nc.vector.tensor_copy(
+            out=w2s[:].rearrange("p (b i q) -> p b i q", b=2, i=4),
+            in_=w2s_raw[:].rearrange("p (b q i) -> p b i q", b=2, i=4),
+        )
+
+        vw = [keep.tile([P, S], U32, name="vw%d" % a, align_bytes=64) for a in range(2)]
+        vs = keep.tile([P, S], U8, name="vs", align_bytes=64)
+        nc.vector.tensor_copy(vw[0][:], tab[0][:].bitcast(U32).indirect(idx[:]))
+        nc.vector.tensor_copy(vs[:], tsc[:].indirect(idx[:]))
+        nc.vector.tensor_copy(vw[1][:], tab[1][:].bitcast(U32).indirect(idx[:]))
+        vw.append(keep.tile([P, S], U32, name="vw2", tag="tsc", align_bytes=64))
+        for hh in range(2):
+            nc.vector.tensor_copy(
+                vw[2][:, 512 * hh : 512 * hh + 512], tab[2][:].bitcast(U32).indirect(idx[:, 32 * hh : 32 * hh + 32])
+            )
+
+        hbuf = {}
+
+        def stage1(k):
+            b, i = divmod(k, 4)
+            for hh in range(2):
+                cols = slice(512 * hh, 512 * hh + 512)
+                d = bank((2 * k + hh) % 8, "d%d_%d" % (k, hh))
+                for a in range(2):
+                    codes, scales = w1q[a, b]
+                    nc.tensor.matmul_mx(
+                        out=d[:],
+                        lhsT=codes[:, 128 * i : 128 * i + 128].bitcast(FP8X4),
+                        lhsT_scale=scales[:, 128 * i : 128 * i + 128],
+                        rhs=vw[a][:, cols].bitcast(FP8X4),
+                        rhs_scale=vs[SCALE_ROW[a] : P, cols],
+                        start=(a == 0),
+                        stop=False,
+                    )
+                nc.tensor.matmul_mx(
+                    out=d[:],
+                    lhsT=w2c[:, 256 * k : 256 * k + 256].bitcast(FP4X4),
+                    lhsT_scale=w2s[:, 128 * k : 128 * k + 128],
+                    rhs=vw[2][:, cols].bitcast(FP8X4),
+                    rhs_scale=vs[:, cols],
+                    start=False,
+                    stop=True,
+                )
+                nc.scalar.activation(
+                    out=hbuf[b][:, S * i + 512 * hh : S * i + 512 * hh + 512],
+                    in_=d[:],
+                    func=TANH,
+                    bias=b1_sb[:, b, i : i + 1],
+                )
+
+        gw = {}
+        gwbuf = [keep.tile([P, S], F32, name="gw%d" % k, align_bytes=64) for k in range(3)]
+
+        def gained(k):
+            b, i = divmod(k, 4)
+            gw[k] = gwbuf[k % 3]
+            nc.scalar.activation(out=gw[k][:], in_=wgs_of[i], func=COPY, scale=gain_sb[:, b, i : i + 1])
+
+        def scatter(k, parts):
+            b, i = divmod(k, 4)
+            w = S // parts
+            for u in range(parts):
+                nc.vector.tensor_tensor(
+                    page[k][:].indirect(idx2[:, u * w // 16 : (u + 1) * w // 16]),
+                    hbuf[b][:, S * i + u * w : S * i + (u + 1) * w],
+                    gw[k][:, u * w : (u + 1) * w],
+                    MULT,
+                )
+
+        def weigh(k):
+            b, i = divmod(k, 4)
+            nc.vector.tensor_tensor(hbuf[b][:, M * i : M * i + M], visb[k][:], wgt_sb[:], MULT)
+
+        def pick(k, dst, m0, w):
+            b, i = divmod(k, 4)
+            nc.vector.tensor_tensor(
+                dst,
+                page[k][:].indirect(idx3[:, m0 // 16 : (m0 + w) // 16]),
+                hbuf[b][:, M * i + m0 : M * i + m0 + w],
+                MULT,
+            )
+
+        hbuf[0] = big("h0", "big0", F32)
+        gained(0)
+        stage1(0)
+        gained(1)
+        for k in range(1, 4):
+            stage1(k)
+        x0 = big("x0", "big2", F32)
+        scatter(0, 2)
+        gained(2)
+        for k in range(4):
+            if k < 2:
+                g = group_w1(gwbuf[k][:].bitcast(BF16), w1_raw[k, 1])
+            weigh(k)
+            visb[4 + k] = load_vis(4 + k)
+            scatter(k + 1, 1)
+            if k < 2:
+                w1q[k, 1] = quantise("w1q%d1" % k, g, 512)
+                gained(k + 3)
+            if k == 1:
+                hbuf[1] = big("h1", "big1", F32)
+                for kk in range(4, 8):
+                    stage1(kk)
+            pick(k, x0[:, M * k : M * k + M], 0, M)
+            if k < 3:
+                page[5 + k] = load_page(5 + k)
+        late = big("late", "big0", F32)
+        w3_raw = [late[:, 2048 * u : 2048 * u + 2048].rearrange("p (j c) -> p j c", j=4) for u in range(2)]
+        for u in range(2):
+            nc.sync.dma_start(out=w3_raw[u], in_=w3[512 * u : 512 * u + 512, :].rearrange("(p j) c -> p j c", j=4))
+
+        x0v = x0[:].rearrange("p (j m) -> p j m", j=4)
+        z0 = []
+        w3q = []
+        gained(5)
+        gained(6)
+        g0 = gwbuf[1][:].bitcast(BF16)
+        weave(nc.scalar.copy, g0, x0v[:, :, 0:512], 512)
+        weigh(4)
+        scatter(5, 1)
+        z0.append(quantise("z0_0", g0, 512))
+        g1 = gwbuf[2][:].bitcast(BF16)
+        weave(nc.scalar.copy, g1, x0v[:, :, 512:1024], 512)
+        gained(7)
+        g3 = [weave(nc.scalar.copy, grouped_tile("g_w3_%d" % u), w3_raw[u], 512) for u in range(2)]
+        weigh(5)
+        scatter(6, 1)
+        z0.append(quantise("z0_1", g1, 512))
+        for u in range(2):
+            w3q.append(quantise("w3q%d" % u, g3[u], 512))
+        weigh(6)
+        scatter(7, 1)
+        weigh(7)
+
+        stage = big("stage", "big2", F32)
+        out_rows = out.rearrange("(nb p) m -> p nb m", p=P)
+        starts = [sum(TAIL[:u]) for u in range(len(TAIL))]
+        accs = []
+        nb0 = 0
+        for u, w in enumerate(TAIL):
+            per = 512 // w
+            banks = [bank(nb0 + v, "o%d_%d" % (u, v)) for v in range(4 // per)]
+            nb0 = nb0 + 4 // per
+            accs.append(banks)
+
+        def last(u, b, codes, scales, c0):
+            w = TAIL[u]
+            per = 512 // w
+            for nb in range(4):
+                wc, ws = w3q[b]
+                nc.tensor.matmul_mx(
+                    out=accs[u][nb // per][:, (nb % per) * w : (nb % per + 1) * w],
+                    lhsT=wc[:, 128 * nb : 128 * nb + 128].bitcast(FP8X4),
+                    lhsT_scale=ws[:, 128 * nb : 128 * nb + 128],
+                    rhs=codes[:, c0 : c0 + w].bitcast(FP8X4),
+                    rhs_scale=scales[:, c0 : c0 + w],
+                    start=(b == 0 and nb % per == 0),
+                    stop=(b == 1 and nb % per == per - 1),
+                )
+
+        for u, w in enumerate(TAIL):
+            codes, scales = z0[starts[u] // 512]
+            last(u, 0, codes, scales, starts[u] % 512)
+
+        xp = {}
+
+        def picks(u):
+            m0, w = starts[u], TAIL[u]
+            if u == 0:
+                xp[u] = gwbuf[1][:].rearrange("p (j m) -> p j m", j=4)
+            elif u == 1:
+                xp[u] = hbuf[1][:].rearrange("p (j m) -> p j m", j=4)[:, :, 0:w]
+            else:
+                xp[u] = late[:, 4 * m0 : 4 * m0 + 4 * w].rearrange("p (j m) -> p j m", j=4)
+            for i in range(4):
+                pick(4 + i, xp[u][:, i, :], m0, w)
+
+        def woven(u):
+            w = TAIL[u]
+            eng = nc.vector.tensor_copy if u == len(TAIL) - 1 else nc.scalar.copy
+            if u + 2 < len(TAIL):
+                g = late[:, 4 * starts[u + 2] : 4 * starts[u + 2] + 2 * w].bitcast(BF16)
+            else:
+                g = grouped_tile("g_z1_%d" % u)
+            return weave(eng, g, xp[u], w)
+
+        def finish(u, g):
+            m0, w = starts[u], TAIL[u]
+            codes, scales = quantise("z1_%d" % u, g, w)
+            last(u, 1, codes, scales, 0)
+            for v, acc in enumerate(accs[u]):
+                eng = nc.vector.tensor_copy if u >= len(TAIL) - 2 else nc.scalar.copy
+                eng(out=stage[:, 4 * m0 + 512 * v : 4 * m0 + 512 * v + 512], in_=acc[:])
+            nc.sync.dma_start(
+                out=out_rows[:, :, m0 : m0 + w],
+                in_=stage[:, 4 * m0 : 4 * m0 + 4 * w].rearrange("p (nb m) -> p nb m", nb=4),
+            )
+
+        picks(0)
+        g_prev = woven(0)
+        for u in range(1, len(TAIL)):
+            picks(u)
+            g_next = woven(u)
+            finish(u - 1, g_prev)
+            g_prev = g_next
+        finish(len(TAIL) - 1, g_prev)

@@ -71,14 +71,14 @@ def tile_list_drone_gate_features_kernel(
 
         def group_w1(g, raw):
             nc.scalar.copy(
-                out=g[:, :].rearrange("p (t m j) -> p m j t", t=4, j=4), in_=raw[:].rearrange("p j (m t) -> p m j t", t=4)
+                out=g[:, :].rearrange("p (t m j) -> p t m j", t=4, j=4), in_=raw[:].rearrange("p j (m t) -> p t m j", t=4)
             )
             return g
 
         def weave(engine_copy, g, planes, width):
             engine_copy(
-                out=g[:, : 4 * width].rearrange("p (c k j) -> p c j k", k=4, j=4),
-                in_=planes.rearrange("p j (c k) -> p c j k", k=4),
+                out=g[:, : 4 * width].rearrange("p (c j) -> p c j", j=4),
+                in_=planes.rearrange("p j c -> p c j"),
             )
             return g
 

@@ -43,15 +43,10 @@ def tile_list_drone_gate_features_kernel(
 
         tsc = keep.tile([P, T], U8, name="tsc", tag="tsc", align_bytes=64)
         w2s_raw = keep.tile([P, H], U8, name="w2s_raw", align_bytes=64)
-        nc.vector.memset(w2s_raw[:].bitcast(I32), 0)
         nc.vector.memset(tsc[:].bitcast(I32), 0)
+        nc.vector.memset(w2s_raw[:].bitcast(I32), 0)
         ts32 = tab_scales.bitcast(I32)
         w2s32 = w2_scales.bitcast(I32)
-        for q in range(4):
-            nc.gpsimd.dma_start(out=w2s_raw[32 * q : 32 * q + 4, :].bitcast(I32), in_=w2s32[0, 4 * q : 4 * q + 4, :])
-        for q in range(4):
-            nc.gpsimd.dma_start(out=tsc[32 * q + 4 : 32 * q + 12, :].bitcast(I32), in_=ts32[0:2, 4 * q : 4 * q + 4, :])
-            nc.gpsimd.dma_start(out=tsc[32 * q : 32 * q + 4, :].bitcast(I32), in_=ts32[2, 4 * q : 4 * q + 4, :])
         b1_sb = keep.tile([P, 2, 4], F32, name="b1_sb")
         gain_sb = keep.tile([P, 2, 4], F32, name="gain_sb")
 
@@ -61,35 +56,33 @@ def tile_list_drone_gate_features_kernel(
             return raw
 
         def grouped_tile(name):
-            return ring.tile([P, 2048], BF16, name=name, tag="grouped", bufs=3, align_bytes=64)
+            return ring.tile([P, 2048], BF16, name=name, tag="grouped", bufs=2, align_bytes=64)
 
-        def quantise(name, grouped, width):
-            codes = keep.tile([P, width], U32, name=name + "_codes", align_bytes=64)
+        def quantise(name, grouped, width, tag=""):
+            codes = keep.tile([P, width], U32, name=name + "_codes", tag=tag, align_bytes=64)
             scales = keep.tile([P, width], U8, name=name + "_scales", align_bytes=64)
             nc.vector.quantize_mx(out=codes[:].bitcast(FP8X4), scales=scales[:], in_=grouped[:, : 4 * width])
             return codes, scales
 
         def group_w1(g, raw):
             nc.scalar.copy(
-                out=g[:, :].rearrange("p (t m j) -> p t m j", t=4, j=4), in_=raw[:].rearrange("p j (m t) -> p t m j", t=4)
+                out=g[:, :].rearrange("p (t m j) -> p m j t", t=4, j=4), in_=raw[:].rearrange("p j (m t) -> p m j t", t=4)
             )
             return g
 
         def weave(engine_copy, g, planes, width):
             engine_copy(
-                out=g[:, : 4 * width].rearrange("p (c j) -> p c j", j=4),
-                in_=planes.rearrange("p j c -> p c j"),
+                out=g[:, : 4 * width].rearrange("p (c k j) -> p c j k", k=4, j=4),
+                in_=planes.rearrange("p j (c k) -> p c j k", k=4),
             )
             return g
 
         wgs_rows = wgs.rearrange("(q i) j -> q i j", i=4)
-        wgs_sb = [keep.tile([P, n, S], F32, name="wgs%d" % k) for k, n in enumerate((1, 1, 2))]
+        wgs_sb = [keep.tile([P, S], F32, name="wgs%d" % i) for i in range(4)]
 
-        def load_wgs(k, i0, i1):
+        def load_wgs(i):
             for a in (0, 2, 1, 3):
-                nc.sync.dma_start(out=wgs_sb[k][32 * a : 32 * a + 32, :, :], in_=wgs_rows[:, i0:i1, :])
-
-        wgs_of = [wgs_sb[0][:, 0, :], wgs_sb[1][:, 0, :], wgs_sb[2][:, 0, :], wgs_sb[2][:, 1, :]]
+                nc.sync.dma_start(out=wgs_sb[i][32 * a : 32 * a + 32, :], in_=wgs_rows[:, i, :])
 
         page_rows = page0.rearrange("(b p i) t -> b i p t", b=2, i=4)
         vis_rows = vis.rearrange("(b p i) m -> b i p m", b=2, i=4)
@@ -100,41 +93,58 @@ def tile_list_drone_gate_features_kernel(
             return t
 
         def load_vis(k):
-            t = ring.tile([P, M], F32, name="vis%d" % k, tag="vis", bufs=4)
+            t = ring.tile([P, M], F32, name="vis%d" % k, tag="vis", bufs=3)
             nc.sync.dma_start(out=t[:], in_=vis_rows[k // 4, k % 4])
             return t
 
         w1_raw = {}
-        for a in range(2):
-            w1_raw[a, 0] = load_w("w1raw%d0" % a, w1[512 * a : 512 * a + 512, 0:512])
-        load_wgs(0, 0, 1)
+        w1_raw[0, 0] = load_w("w1raw00", w1[0:512, 0:512])
         w2_raw = keep.tile([P, 2 * H], U8, name="w2_raw", align_bytes=64)
         nc.sync.dma_start(out=w2_raw[:].bitcast(I32), in_=w2_words[0].bitcast(I32))
         nc.sync.dma_start(idx[:], offs)
-        tab = []
-        for a in range(3):
-            t = big("tab%d" % a, "big%d" % a, I32)
-            nc.sync.dma_start(out=t[:], in_=tab_words[a].rearrange("p t i -> p (t i)").bitcast(I32))
-            tab.append(t)
-            if a == 0:
-                nc.sync.dma_start(out=gain_sb[:], in_=gain.rearrange("(b p i) -> p b i", b=2, i=4))
+        load_wgs(0)
+        w1_raw[1, 0] = load_w("w1raw10", w1[512:1024, 0:512])
+        tab = [big("tab%d" % a, "big%d" % a, I32) for a in range(3)]
+
+        def load_tab(a, half):
+            cols = slice(half * T // 2, (half + 1) * T // 2)
+            nc.sync.dma_start(out=tab[a][:, cols], in_=tab_words[a].rearrange("p t i -> p (t i)").bitcast(I32)[:, cols])
+
+        def load_tab_scales(q):
+            nc.sync.dma_start(out=tsc[32 * q + 4 : 32 * q + 12, :].bitcast(I32), in_=ts32[0:2, 4 * q : 4 * q + 4, :])
+            nc.sync.dma_start(out=tsc[32 * q : 32 * q + 4, :].bitcast(I32), in_=ts32[2, 4 * q : 4 * q + 4, :])
+
+        load_tab(0, 0)
+        for q in range(3):
+            load_tab_scales(q)
+        load_tab(0, 1)
+        load_tab_scales(3)
+        load_tab(1, 0)
+        for q in range(4):
+            nc.sync.dma_start(out=w2s_raw[32 * q : 32 * q + 4, :].bitcast(I32), in_=w2s32[0, 4 * q : 4 * q + 4, :])
+        load_tab(1, 1)
+        nc.sync.dma_start(out=gain_sb[:], in_=gain.rearrange("(b p i) -> p b i", b=2, i=4))
         nc.sync.dma_start(out=b1_sb[:], in_=b1.rearrange("(b p i) -> p b i", b=2, i=4))
+        load_tab(2, 0)
         nc.sync.dma_start(idx2[:], offs2)
         nc.sync.dma_start(idx3[:], offs3)
+        load_tab(2, 1)
         page = {0: load_page(0)}
-        load_wgs(1, 1, 2)
+        load_wgs(1)
         page[1] = load_page(1)
+        load_wgs(2)
         wgt_sb = keep.tile([P, M], F32, name="wgt_sb")
         nc.sync.dma_start(out=wgt_sb[:], in_=wgt)
         visb = {0: load_vis(0)}
-        load_wgs(2, 2, 4)
+        load_wgs(3)
         page[2] = load_page(2)
         for a in range(2):
             w1_raw[a, 1] = load_w("w1raw%d1" % a, w1[512 * a : 512 * a + 512, 512:1024])
         visb[1] = load_vis(1)
         page[3] = load_page(3)
         visb[2] = load_vis(2)
-        visb[3] = load_vis(3)
+        w3_raw = [load_w("w3raw0", w3[0:512, :])]
+        w3_raw.append(load_w("w3raw1", w3[512:1024, :]))
         page[4] = load_page(4)
 
         w2c = keep.tile([P, 2 * H], U8, name="w2c", align_bytes=64)
@@ -196,90 +206,101 @@ def tile_list_drone_gate_features_kernel(
                     bias=b1_sb[:, b, i : i + 1],
                 )
 
-        gw = {}
-        gwbuf = [keep.tile([P, S], F32, name="gw%d" % k, align_bytes=64) for k in range(3)]
+        gw = keep.tile([P, S], F32, name="gw")
+        prod = {}
+        wv = {}
+
+        def region(k):
+            return hbuf[k // 4][:, S * (k % 4) : S * (k % 4) + S]
 
         def gained(k):
             b, i = divmod(k, 4)
-            gw[k] = gwbuf[k % 3]
-            nc.scalar.activation(out=gw[k][:], in_=wgs_of[i], func=COPY, scale=gain_sb[:, b, i : i + 1])
+            nc.scalar.activation(out=gw[:], in_=wgs_sb[i][:], func=COPY, scale=gain_sb[:, b, i : i + 1])
 
-        def scatter(k, parts):
-            b, i = divmod(k, 4)
-            w = S // parts
-            for u in range(parts):
-                nc.vector.tensor_tensor(
-                    page[k][:].indirect(idx2[:, u * w // 16 : (u + 1) * w // 16]),
-                    hbuf[b][:, S * i + u * w : S * i + (u + 1) * w],
-                    gw[k][:, u * w : (u + 1) * w],
-                    MULT,
-                )
+        def product(k, dst):
+            nc.gpsimd.tensor_tensor(dst, region(k), gw[:], MULT)
+            prod[k] = dst
+            if k < 7:
+                gained(k + 1)
 
-        def weigh(k):
-            b, i = divmod(k, 4)
-            nc.vector.tensor_tensor(hbuf[b][:, M * i : M * i + M], visb[k][:], wgt_sb[:], MULT)
+        def scatter(k, j0, w):
+            nc.vector.tensor_copy(page[k][:].indirect(idx2[:, j0 // 16 : (j0 + w) // 16]), prod[k][:, j0 : j0 + w])
+
+        def weigh(k, dst):
+            nc.gpsimd.tensor_tensor(dst, visb[k][:], wgt_sb[:], MULT)
+            wv[k] = dst
+            if k < 5:
+                visb[k + 3] = load_vis(k + 3)
 
         def pick(k, dst, m0, w):
-            b, i = divmod(k, 4)
             nc.vector.tensor_tensor(
-                dst,
-                page[k][:].indirect(idx3[:, m0 // 16 : (m0 + w) // 16]),
-                hbuf[b][:, M * i + m0 : M * i + m0 + w],
-                MULT,
+                dst, page[k][:].indirect(idx3[:, m0 // 16 : (m0 + w) // 16]), wv[k][:, m0 : m0 + w], MULT
             )
 
         hbuf[0] = big("h0", "big0", F32)
-        gained(0)
-        stage1(0)
-        gained(1)
-        for k in range(1, 4):
-            stage1(k)
+        hbuf[1] = big("h1", "big1", F32)
         x0 = big("x0", "big2", F32)
-        scatter(0, 2)
-        gained(2)
+        spare = keep.tile([P, S], F32, name="spare")
+        gained(0)
         for k in range(4):
-            if k < 2:
-                g = group_w1(gwbuf[k][:].bitcast(BF16), w1_raw[k, 1])
-            weigh(k)
-            visb[4 + k] = load_vis(4 + k)
-            scatter(k + 1, 1)
-            if k < 2:
-                w1q[k, 1] = quantise("w1q%d1" % k, g, 512)
-                gained(k + 3)
-            if k == 1:
-                hbuf[1] = big("h1", "big1", F32)
-                for kk in range(4, 8):
-                    stage1(kk)
+            stage1(k)
+        prod[0] = region(0)
+        nc.vector.tensor_tensor(prod[0][:, 0:512], prod[0][:, 0:512], gw[:, 0:512], MULT)
+        nc.gpsimd.tensor_tensor(prod[0][:, 512:S], prod[0][:, 512:S], gw[:, 512:S], MULT)
+        gained(1)
+        scatter(0, 0, 512)
+        scatter(0, 512, 512)
+        product(1, spare[:])
+        scatter(1, 0, S)
+        product(2, region(1))
+        weigh(0, region(2))
+
+        def pick_whole(k):
             pick(k, x0[:, M * k : M * k + M], 0, M)
             if k < 3:
                 page[5 + k] = load_page(5 + k)
-        late = big("late", "big0", F32)
-        w3_raw = [late[:, 2048 * u : 2048 * u + 2048].rearrange("p (j c) -> p j c", j=4) for u in range(2)]
-        for u in range(2):
-            nc.sync.dma_start(out=w3_raw[u], in_=w3[512 * u : 512 * u + 512, :].rearrange("(p j) c -> p j c", j=4))
 
-        x0v = x0[:].rearrange("p (j m) -> p j m", j=4)
-        z0 = []
-        w3q = []
-        gained(5)
-        gained(6)
-        g0 = gwbuf[1][:].bitcast(BF16)
-        weave(nc.scalar.copy, g0, x0v[:, :, 0:512], 512)
-        weigh(4)
-        scatter(5, 1)
-        z0.append(quantise("z0_0", g0, 512))
-        g1 = gwbuf[2][:].bitcast(BF16)
-        weave(nc.scalar.copy, g1, x0v[:, :, 512:1024], 512)
-        gained(7)
-        g3 = [weave(nc.scalar.copy, grouped_tile("g_w3_%d" % u), w3_raw[u], 512) for u in range(2)]
-        weigh(5)
-        scatter(6, 1)
-        z0.append(quantise("z0_1", g1, 512))
+        pick_whole(0)
+        scatter(2, 0, S)
+        product(3, region(2))
+        weigh(1, region(3))
+        g1 = x0[:, M : 3 * M].bitcast(BF16)
+        for a in range(2):
+            group_w1(g1[:, 2048 * a : 2048 * a + 2048], w1_raw[a, 1])
+        codes, scales = quantise("w1q_1", g1, 1024)
+        for a in range(2):
+            w1q[a, 1] = (codes[:, 512 * a : 512 * a + 512], scales[:, 512 * a : 512 * a + 512])
+        for k in range(4, 8):
+            stage1(k)
+        pick_whole(1)
+        scatter(3, 0, S)
+        weigh(2, region(3))
+        product(4, region(4))
+        g3 = x0[:, 2 * M : 4 * M].bitcast(BF16)
         for u in range(2):
-            w3q.append(quantise("w3q%d" % u, g3[u], 512))
-        weigh(6)
-        scatter(7, 1)
-        weigh(7)
+            weave(nc.scalar.copy, g3[:, 2048 * u : 2048 * u + 2048], w3_raw[u][:], 512)
+        codes, scales = quantise("w3q", g3, 1024)
+        w3q = [(codes[:, 512 * u : 512 * u + 512], scales[:, 512 * u : 512 * u + 512]) for u in range(2)]
+        pick_whole(2)
+        scatter(4, 0, S)
+        product(5, region(3))
+        weigh(3, region(5))
+        pick_whole(3)
+        scatter(5, 0, S)
+        product(6, region(5))
+        weigh(4, region(6))
+        last_prod = keep.tile([P, S], F32, name="last_prod", tag="last_prod", align_bytes=64)
+        product(7, last_prod[:])
+        weigh(5, region(7))
+        wide = keep.tile([P, 2048], F32, name="wide", align_bytes=64)
+        x0v = x0[:].rearrange("p (j m) -> p j m", j=4)
+        for u in range(2):
+            weave(nc.scalar.copy, wide[:, M * u : M * u + M].bitcast(BF16), x0v[:, :, 512 * u : 512 * u + 512], 512)
+        scatter(6, 0, S)
+        weigh(6, region(3))
+        scatter(7, 0, S)
+        weigh(7, region(5))
+        z0 = quantise("z0", wide[:].bitcast(BF16), 1024, tag="last_prod")
 
         stage = big("stage", "big2", F32)
         out_rows = out.rearrange("(nb p) m -> p nb m", p=P)
@@ -308,19 +329,16 @@ def tile_list_drone_gate_features_kernel(
                 )
 
         for u, w in enumerate(TAIL):
-            codes, scales = z0[starts[u] // 512]
-            last(u, 0, codes, scales, starts[u] % 512)
+            last(u, 0, z0[0], z0[1], starts[u])
 
         xp = {}
 
         def picks(u):
             m0, w = starts[u], TAIL[u]
-            if u == 0:
-                xp[u] = gwbuf[1][:].rearrange("p (j m) -> p j m", j=4)
-            elif u == 1:
-                xp[u] = hbuf[1][:].rearrange("p (j m) -> p j m", j=4)[:, :, 0:w]
+            if u < 2:
+                xp[u] = wide[:, 4 * m0 : 4 * m0 + 4 * w].rearrange("p (j m) -> p j m", j=4)
             else:
-                xp[u] = late[:, 4 * m0 : 4 * m0 + 4 * w].rearrange("p (j m) -> p j m", j=4)
+                xp[u] = hbuf[0][:, 4 * m0 - 2048 : 4 * m0 - 2048 + 4 * w].rearrange("p (j m) -> p j m", j=4)
             for i in range(4):
                 pick(4 + i, xp[u][:, i, :], m0, w)
 
@@ -328,7 +346,7 @@ def tile_list_drone_gate_features_kernel(
             w = TAIL[u]
             eng = nc.vector.tensor_copy if u == len(TAIL) - 1 else nc.scalar.copy
             if u + 2 < len(TAIL):
-                g = late[:, 4 * starts[u + 2] : 4 * starts[u + 2] + 2 * w].bitcast(BF16)
+                g = hbuf[0][:, 4 * starts[u + 2] - 2048 : 4 * starts[u + 2] - 2048 + 2 * w].bitcast(BF16)
             else:
                 g = grouped_tile("g_z1_%d" % u)
             return weave(eng, g, xp[u], w)

@@ -51,7 +51,7 @@ def tile_list_drone_gate_features_kernel(
         gain_sb = keep.tile([P, 2, 4], F32, name="gain_sb")
 
         def load_w(name, rows):
-            raw = ring.tile([P, 4, 512], F32, name=name, tag="wraw", bufs=2)
+            raw = ring.tile([P, 4, 512], F32, name=name, tag="wraw", bufs=3)
             nc.sync.dma_start(out=raw[:], in_=rows.rearrange("(p j) c -> p j c", j=4))
             return raw
 
@@ -59,7 +59,7 @@ def tile_list_drone_gate_features_kernel(
             return ring.tile([P, 2048], BF16, name=name, tag="grouped", bufs=2, align_bytes=64)
 
         def quantise(name, grouped, width, tag=""):
-            codes = keep.tile([P, width], U32, name=name + "_codes", tag=tag, align_bytes=64)
+            codes = ring.tile([P, width], U32, name=name + "_codes", tag=tag, align_bytes=64)
             scales = keep.tile([P, width], U8, name=name + "_scales", align_bytes=64)
             nc.vector.quantize_mx(out=codes[:].bitcast(FP8X4), scales=scales[:], in_=grouped[:, : 4 * width])
             return codes, scales
@@ -93,7 +93,7 @@ def tile_list_drone_gate_features_kernel(
             return t
 
         def load_vis(k):
-            t = ring.tile([P, M], F32, name="vis%d" % k, tag="vis", bufs=3)
+            t = ring.tile([P, M], F32, name="vis%d" % k, tag="vis%d" % (k % 4), align_bytes=64)
             nc.sync.dma_start(out=t[:], in_=vis_rows[k // 4, k % 4])
             return t
 
@@ -141,11 +141,11 @@ def tile_list_drone_gate_features_kernel(
         for a in range(2):
             w1_raw[a, 1] = load_w("w1raw%d1" % a, w1[512 * a : 512 * a + 512, 512:1024])
         visb[1] = load_vis(1)
-        page[3] = load_page(3)
         visb[2] = load_vis(2)
-        w3_raw = [load_w("w3raw0", w3[0:512, :])]
-        w3_raw.append(load_w("w3raw1", w3[512:1024, :]))
+        visb[3] = load_vis(3)
+        page[3] = load_page(3)
         page[4] = load_page(4)
+        w3_raw = [load_w("w3raw%d" % u, w3[512 * u : 512 * u + 512, :]) for u in range(2)]
 
         w2c = keep.tile([P, 2 * H], U8, name="w2c", align_bytes=64)
         w2s = keep.tile([P, H], U8, name="w2s", align_bytes=64)
@@ -207,100 +207,93 @@ def tile_list_drone_gate_features_kernel(
                 )
 
         gw = keep.tile([P, S], F32, name="gw")
+        gw_late = w1_raw[1, 1][:].rearrange("p j c -> p (j c)")[:, 0:S]
         prod = {}
-        wv = {}
 
         def region(k):
             return hbuf[k // 4][:, S * (k % 4) : S * (k % 4) + S]
 
-        def gained(k):
+        def gained(k, dst):
             b, i = divmod(k, 4)
-            nc.scalar.activation(out=gw[:], in_=wgs_sb[i][:], func=COPY, scale=gain_sb[:, b, i : i + 1])
+            nc.scalar.activation(out=dst, in_=wgs_sb[i][:], func=COPY, scale=gain_sb[:, b, i : i + 1])
 
         def product(k, dst):
-            nc.gpsimd.tensor_tensor(dst, region(k), gw[:], MULT)
+            nc.gpsimd.tensor_tensor(dst, region(k), gw[:] if k < 4 else gw_late, MULT)
             prod[k] = dst
-            if k < 7:
-                gained(k + 1)
+            if k == 2:
+                gained(3, gw[:])
+            if 4 <= k < 7:
+                gained(k + 1, gw_late)
 
         def scatter(k, j0, w):
             nc.vector.tensor_copy(page[k][:].indirect(idx2[:, j0 // 16 : (j0 + w) // 16]), prod[k][:, j0 : j0 + w])
 
-        def weigh(k, dst):
-            nc.gpsimd.tensor_tensor(dst, visb[k][:], wgt_sb[:], MULT)
-            wv[k] = dst
-            if k < 5:
-                visb[k + 3] = load_vis(k + 3)
+        def weigh(engine, k, dst, m0, w):
+            engine.tensor_tensor(dst, visb[k][:, m0 : m0 + w], wgt_sb[:, m0 : m0 + w], MULT)
 
-        def pick(k, dst, m0, w):
-            nc.vector.tensor_tensor(
-                dst, page[k][:].indirect(idx3[:, m0 // 16 : (m0 + w) // 16]), wv[k][:, m0 : m0 + w], MULT
-            )
+        def pick(k, dst, m0, w, factor):
+            nc.vector.tensor_tensor(dst, page[k][:].indirect(idx3[:, m0 // 16 : (m0 + w) // 16]), factor, MULT)
 
         hbuf[0] = big("h0", "big0", F32)
         hbuf[1] = big("h1", "big1", F32)
         x0 = big("x0", "big2", F32)
-        spare = keep.tile([P, S], F32, name="spare")
-        gained(0)
-        for k in range(4):
+        wide = keep.tile([P, 2048], F32, name="wide", align_bytes=64)
+        wv_left = keep.tile([P, 512], F32, name="wv_left")
+        gained(0, gw[:])
+        for k in range(2):
+            stage1(k)
+        gained(1, wide[:, 0:S])
+        for k in range(2, 4):
             stage1(k)
         prod[0] = region(0)
+        prod[1] = region(1)
         nc.vector.tensor_tensor(prod[0][:, 0:512], prod[0][:, 0:512], gw[:, 0:512], MULT)
         nc.gpsimd.tensor_tensor(prod[0][:, 512:S], prod[0][:, 512:S], gw[:, 512:S], MULT)
-        gained(1)
+        nc.gpsimd.tensor_tensor(prod[1], prod[1], wide[:, 0:S], MULT)
+        gained(2, gw[:])
         scatter(0, 0, 512)
         scatter(0, 512, 512)
-        product(1, spare[:])
-        scatter(1, 0, S)
-        product(2, region(1))
-        weigh(0, region(2))
-
-        def pick_whole(k):
-            pick(k, x0[:, M * k : M * k + M], 0, M)
+        for k in range(4):
+            weigh(nc.gpsimd, k, wv_left[:], 0, 512)
+            product(k + 2, region((0, 1, 0, 4)[k]))
+            scatter(k + 1, 0, S)
+            wv_right = region((1, 0, 4, 0)[k])[:, 0:512]
+            weigh(nc.vector, k, wv_right, 512, 512)
+            visb[k + 4] = load_vis(k + 4)
+            if k == 1:
+                g1 = x0[:, M : 3 * M].bitcast(BF16)
+                for a in range(2):
+                    group_w1(g1[:, 2048 * a : 2048 * a + 2048], w1_raw[a, 1])
+                gained(4, gw_late)
+                codes, scales = quantise("w1q_1", g1, 1024)
+                for a in range(2):
+                    w1q[a, 1] = (codes[:, 512 * a : 512 * a + 512], scales[:, 512 * a : 512 * a + 512])
+                for kk in range(4, 8):
+                    stage1(kk)
+            pick(k, x0[:, M * k : M * k + 512], 0, 512, wv_left[:])
+            pick(k, x0[:, M * k + 512 : M * k + M], 512, 512, wv_right)
             if k < 3:
                 page[5 + k] = load_page(5 + k)
-
-        pick_whole(0)
-        scatter(2, 0, S)
-        product(3, region(2))
-        weigh(1, region(3))
-        g1 = x0[:, M : 3 * M].bitcast(BF16)
-        for a in range(2):
-            group_w1(g1[:, 2048 * a : 2048 * a + 2048], w1_raw[a, 1])
-        codes, scales = quantise("w1q_1", g1, 1024)
-        for a in range(2):
-            w1q[a, 1] = (codes[:, 512 * a : 512 * a + 512], scales[:, 512 * a : 512 * a + 512])
-        for k in range(4, 8):
-            stage1(k)
-        pick_whole(1)
-        scatter(3, 0, S)
-        weigh(2, region(3))
-        product(4, region(4))
-        g3 = x0[:, 2 * M : 4 * M].bitcast(BF16)
+        g3 = hbuf[0][:, 2 * S : 4 * S].bitcast(BF16)
         for u in range(2):
             weave(nc.scalar.copy, g3[:, 2048 * u : 2048 * u + 2048], w3_raw[u][:], 512)
-        codes, scales = quantise("w3q", g3, 1024)
-        w3q = [(codes[:, 512 * u : 512 * u + 512], scales[:, 512 * u : 512 * u + 512]) for u in range(2)]
-        pick_whole(2)
-        scatter(4, 0, S)
-        product(5, region(3))
-        weigh(3, region(5))
-        pick_whole(3)
+        product(6, region(0))
         scatter(5, 0, S)
-        product(6, region(5))
-        weigh(4, region(6))
-        last_prod = keep.tile([P, S], F32, name="last_prod", tag="last_prod", align_bytes=64)
+        last_prod = keep.tile([P, S], F32, name="last_prod")
         product(7, last_prod[:])
-        weigh(5, region(7))
-        wide = keep.tile([P, 2048], F32, name="wide", align_bytes=64)
+        wv = {4: region(6), 5: region(7), 6: region(0), 7: last_prod[:]}
+        weigh(nc.gpsimd, 4, wv[4], 0, M)
+        weigh(nc.gpsimd, 5, wv[5], 0, M)
         x0v = x0[:].rearrange("p (j m) -> p j m", j=4)
         for u in range(2):
             weave(nc.scalar.copy, wide[:, M * u : M * u + M].bitcast(BF16), x0v[:, :, 512 * u : 512 * u + 512], 512)
         scatter(6, 0, S)
-        weigh(6, region(3))
+        weigh(nc.gpsimd, 6, wv[6], 0, M)
         scatter(7, 0, S)
-        weigh(7, region(5))
-        z0 = quantise("z0", wide[:].bitcast(BF16), 1024, tag="last_prod")
+        weigh(nc.vector, 7, wv[7], 0, M)
+        codes, scales = quantise("w3q", g3, 1024, tag="vis1")
+        w3q = [(codes[:, 512 * u : 512 * u + 512], scales[:, 512 * u : 512 * u + 512]) for u in range(2)]
+        z0 = quantise("z0", wide[:].bitcast(BF16), 1024, tag="vis2")
 
         stage = big("stage", "big2", F32)
         out_rows = out.rearrange("(nb p) m -> p nb m", p=P)
@@ -338,15 +331,15 @@ def tile_list_drone_gate_features_kernel(
             if u < 2:
                 xp[u] = wide[:, 4 * m0 : 4 * m0 + 4 * w].rearrange("p (j m) -> p j m", j=4)
             else:
-                xp[u] = hbuf[0][:, 4 * m0 - 2048 : 4 * m0 - 2048 + 4 * w].rearrange("p (j m) -> p j m", j=4)
+                xp[u] = hbuf[0][:, 4 * m0 : 4 * m0 + 4 * w].rearrange("p (j m) -> p j m", j=4)
             for i in range(4):
-                pick(4 + i, xp[u][:, i, :], m0, w)
+                pick(4 + i, xp[u][:, i, :], m0, w, wv[4 + i][:, m0 : m0 + w])
 
         def woven(u):
             w = TAIL[u]
             eng = nc.vector.tensor_copy if u == len(TAIL) - 1 else nc.scalar.copy
             if u + 2 < len(TAIL):
-                g = hbuf[0][:, 4 * starts[u + 2] - 2048 : 4 * starts[u + 2] - 2048 + 2 * w].bitcast(BF16)
+                g = hbuf[0][:, 4 * starts[u + 2] : 4 * starts[u + 2] + 2 * w].bitcast(BF16)
             else:
                 g = grouped_tile("g_z1_%d" % u)
             return weave(eng, g, xp[u], w)

from contextlib import ExitStack

import concourse.mybir as mybir

F32 = mybir.dt.float32
BF16 = mybir.dt.bfloat16
I32 = mybir.dt.int32
U32 = mybir.dt.uint32
U16 = mybir.dt.uint16
U8 = mybir.dt.uint8
FP8X4 = mybir.dt.float8_e4m3fn_x4
FP4X4 = mybir.dt.float4_e2m1fn_x4
MULT = mybir.AluOpType.mult
COPY = mybir.ActivationFunctionType.Copy
TANH = mybir.ActivationFunctionType.Tanh

T, S, H, N, T2, M = 4096, 1024, 1024, 512, 2048, 1024
P = 128
FLOPS = 2 * 1536 * H * S + 2 * H * N * M
SCALE_ROW = (4, 8, 0)
TAIL = (256, 256, 256, 128, 128)


def tile_list_drone_gate_features_kernel(
    tc, tab_words, tab_scales, offs, w1, w2_words, w2_scales, b1, gain, wgs, page0, offs2, wgt, offs3, vis, w3, out
):
    nc = tc.nc
    with ExitStack() as ctx:
        lists = ctx.enter_context(tc.tile_pool(name="lists", bufs=1))
        keep = ctx.enter_context(tc.tile_pool(name="keep", bufs=1))
        ring = ctx.enter_context(tc.tile_pool(name="ring", bufs=1))
        psum = ctx.enter_context(tc.psum_pool(name="psum", bufs=1))

        idx = lists.tile([P, S // 16], U16, name="idx")
        idx2 = lists.tile([P, S // 16], U16, name="idx2")
        idx3 = lists.tile([P, M // 16], U16, name="idx3")

        def big(name, tag, dtype):
            return keep.tile([P, 4096], dtype, name=name, tag=tag, align_bytes=64)

        def bank(k, name):
            return psum.tile([P, 512], F32, name=name, tag="bank%d" % k)

        tsc = keep.tile([P, T], U8, name="tsc", tag="tsc", align_bytes=64)
        w2s_raw = keep.tile([P, H], U8, name="w2s_raw", align_bytes=64)
        nc.vector.memset(tsc[:].bitcast(I32), 0)
        nc.vector.memset(w2s_raw[:].bitcast(I32), 0)
        ts32 = tab_scales.bitcast(I32)
        w2s32 = w2_scales.bitcast(I32)
        b1_sb = keep.tile([P, 2, 4], F32, name="b1_sb")
        gain_sb = keep.tile([P, 2, 4], F32, name="gain_sb")

        def load_w(name, rows):
            raw = ring.tile([P, 4, 512], F32, name=name, tag="wraw", bufs=3)
            nc.sync.dma_start(out=raw[:], in_=rows.rearrange("(p j) c -> p j c", j=4))
            return raw

        def grouped_tile(name):
            return ring.tile([P, 2048], BF16, name=name, tag="grouped", bufs=2, align_bytes=64)

        def quantise(name, grouped, width, tag=""):
            codes = ring.tile([P, width], U32, name=name + "_codes", tag=tag, align_bytes=64)
            scales = keep.tile([P, width], U8, name=name + "_scales", align_bytes=64)
            nc.vector.quantize_mx(out=codes[:].bitcast(FP8X4), scales=scales[:], in_=grouped[:, : 4 * width])
            return codes, scales

        def group_w1(g, raw):
            nc.scalar.copy(
                out=g[:, :].rearrange("p (t m j) -> p m j t", t=4, j=4), in_=raw[:].rearrange("p j (m t) -> p m j t", t=4)
            )
            return g

        def weave(engine_copy, g, planes, width):
            engine_copy(
                out=g[:, : 4 * width].rearrange("p (c k j) -> p c j k", k=4, j=4),
                in_=planes.rearrange("p j (c k) -> p c j k", k=4),
            )
            return g

        wgs_rows = wgs.rearrange("(q i) j -> q i j", i=4)
        wgs_sb = [keep.tile([P, S], F32, name="wgs%d" % i) for i in range(4)]

        def load_wgs(i):
            for a in (0, 2, 1, 3):
                nc.sync.dma_start(out=wgs_sb[i][32 * a : 32 * a + 32, :], in_=wgs_rows[:, i, :])

        page_rows = page0.rearrange("(b p i) t -> b i p t", b=2, i=4)
        vis_rows = vis.rearrange("(b p i) m -> b i p m", b=2, i=4)

        def load_page(k):
            t = ring.tile([P, T2], F32, name="page%d" % k, tag="page", bufs=5)
            nc.sync.dma_start(out=t[:], in_=page_rows[k // 4, k % 4])
            return t

        def load_vis(k):
            t = ring.tile([P, M], F32, name="vis%d" % k, tag="vis%d" % (k % 4), align_bytes=64)
            nc.sync.dma_start(out=t[:], in_=vis_rows[k // 4, k % 4])
            return t

        w1_raw = {}
        w1_raw[0, 0] = load_w("w1raw00", w1[0:512, 0:512])
        w2_raw = keep.tile([P, 2 * H], U8, name="w2_raw", align_bytes=64)
        nc.sync.dma_start(out=w2_raw[:].bitcast(I32), in_=w2_words[0].bitcast(I32))
        nc.sync.dma_start(idx[:], offs)
        load_wgs(0)
        w1_raw[1, 0] = load_w("w1raw10", w1[512:1024, 0:512])
        tab = [big("tab%d" % a, "big%d" % a, I32) for a in range(3)]

        def load_tab(a, half):
            cols = slice(half * T // 2, (half + 1) * T // 2)
            nc.sync.dma_start(out=tab[a][:, cols], in_=tab_words[a].rearrange("p t i -> p (t i)").bitcast(I32)[:, cols])

        def load_tab_scales(q):
            nc.sync.dma_start(out=tsc[32 * q + 4 : 32 * q + 12, :].bitcast(I32), in_=ts32[0:2, 4 * q : 4 * q + 4, :])
            nc.sync.dma_start(out=tsc[32 * q : 32 * q + 4, :].bitcast(I32), in_=ts32[2, 4 * q : 4 * q + 4, :])

        load_tab(0, 0)
        for q in range(3):
            load_tab_scales(q)
        load_tab(0, 1)
        load_tab_scales(3)
        load_tab(1, 0)
        for q in range(4):
            nc.sync.dma_start(out=w2s_raw[32 * q : 32 * q + 4, :].bitcast(I32), in_=w2s32[0, 4 * q : 4 * q + 4, :])
        load_tab(1, 1)
        nc.sync.dma_start(out=gain_sb[:], in_=gain.rearrange("(b p i) -> p b i", b=2, i=4))
        nc.sync.dma_start(out=b1_sb[:], in_=b1.rearrange("(b p i) -> p b i", b=2, i=4))
        load_tab(2, 0)
        nc.sync.dma_start(idx2[:], offs2)
        nc.sync.dma_start(idx3[:], offs3)
        load_tab(2, 1)
        page = {0: load_page(0)}
        load_wgs(1)
        page[1] = load_page(1)
        load_wgs(2)
        wgt_sb = keep.tile([P, M], F32, name="wgt_sb")
        nc.sync.dma_start(out=wgt_sb[:], in_=wgt)
        visb = {0: load_vis(0)}
        load_wgs(3)
        page[2] = load_page(2)
        for a in range(2):
            w1_raw[a, 1] = load_w("w1raw%d1" % a, w1[512 * a : 512 * a + 512, 512:1024])
        visb[1] = load_vis(1)
        visb[2] = load_vis(2)
        visb[3] = load_vis(3)
        page[3] = load_page(3)
        page[4] = load_page(4)
        w3_raw = [load_w("w3raw%d" % u, w3[512 * u : 512 * u + 512, :]) for u in range(2)]

        w2c = keep.tile([P, 2 * H], U8, name="w2c", align_bytes=64)
        w2s = keep.tile([P, H], U8, name="w2s", align_bytes=64)
        nc.vector.tensor_copy(
            out=w2c[:].rearrange("p (b i q e) -> p b i q e", b=2, i=4, e=2),
            in_=w2_raw[:].rearrange("p (b q i e) -> p b i q e", b=2, i=4, e=2),
        )
        w1q = {}
        for a in range(2):
            w1q[a, 0] = quantise("w1q%d0" % a, group_w1(grouped_tile("g_w1_%d0" % a), w1_raw[a, 0]), 512)
        nc.vector.tensor_copy(
            out=w2s[:].rearrange("p (b i q) -> p b i q", b=2, i=4),
            in_=w2s_raw[:].rearrange("p (b q i) -> p b i q", b=2, i=4),
        )

        vw = [keep.tile([P, S], U32, name="vw%d" % a, align_bytes=64) for a in range(2)]
        vs = keep.tile([P, S], U8, name="vs", align_bytes=64)
        nc.vector.tensor_copy(vw[0][:], tab[0][:].bitcast(U32).indirect(idx[:]))
        nc.vector.tensor_copy(vs[:], tsc[:].indirect(idx[:]))
        nc.vector.tensor_copy(vw[1][:], tab[1][:].bitcast(U32).indirect(idx[:]))
        vw.append(keep.tile([P, S], U32, name="vw2", tag="tsc", align_bytes=64))
        for hh in range(2):
            nc.vector.tensor_copy(
                vw[2][:, 512 * hh : 512 * hh + 512], tab[2][:].bitcast(U32).indirect(idx[:, 32 * hh : 32 * hh + 32])
            )

        hbuf = {}

        def stage1(k):
            b, i = divmod(k, 4)
            for hh in range(2):
                cols = slice(512 * hh, 512 * hh + 512)
                d = bank((2 * k + hh) % 8, "d%d_%d" % (k, hh))
                for a in range(2):
                    codes, scales = w1q[a, b]
                    nc.tensor.matmul_mx(
                        out=d[:],
                        lhsT=codes[:, 128 * i : 128 * i + 128].bitcast(FP8X4),
                        lhsT_scale=scales[:, 128 * i : 128 * i + 128],
                        rhs=vw[a][:, cols].bitcast(FP8X4),
                        rhs_scale=vs[SCALE_ROW[a] : P, cols],
                        start=(a == 0),
                        stop=False,
                    )
                nc.tensor.matmul_mx(
                    out=d[:],
                    lhsT=w2c[:, 256 * k : 256 * k + 256].bitcast(FP4X4),
                    lhsT_scale=w2s[:, 128 * k : 128 * k + 128],
                    rhs=vw[2][:, cols].bitcast(FP8X4),
                    rhs_scale=vs[:, cols],
                    start=False,
                    stop=True,
                )
                nc.scalar.activation(
                    out=hbuf[b][:, S * i + 512 * hh : S * i + 512 * hh + 512],
                    in_=d[:],
                    func=TANH,
                    bias=b1_sb[:, b, i : i + 1],
                )

        gw = keep.tile([P, S], F32, name="gw")
        gw_late = w1_raw[1, 1][:].rearrange("p j c -> p (j c)")[:, 0:S]
        prod = {}

        def region(k):
            return hbuf[k // 4][:, S * (k % 4) : S * (k % 4) + S]

        def gained(k, dst):
            b, i = divmod(k, 4)
            nc.scalar.activation(out=dst, in_=wgs_sb[i][:], func=COPY, scale=gain_sb[:, b, i : i + 1])

        def product(k, dst):
            nc.gpsimd.tensor_tensor(dst, region(k), gw[:] if k < 4 else gw_late, MULT)
            prod[k] = dst
            if k == 2:
                gained(3, gw[:])
            if 4 <= k < 7:
                gained(k + 1, gw_late)

        def scatter(k, j0, w):
            nc.vector.tensor_copy(page[k][:].indirect(idx2[:, j0 // 16 : (j0 + w) // 16]), prod[k][:, j0 : j0 + w])

        def weigh(engine, k, dst, m0, w):
            engine.tensor_tensor(dst, visb[k][:, m0 : m0 + w], wgt_sb[:, m0 : m0 + w], MULT)

        def pick(k, dst, m0, w, factor):
            nc.vector.tensor_tensor(dst, page[k][:].indirect(idx3[:, m0 // 16 : (m0 + w) // 16]), factor, MULT)

        hbuf[0] = big("h0", "big0", F32)
        hbuf[1] = big("h1", "big1", F32)
        x0 = big("x0", "big2", F32)
        wide = keep.tile([P, 2048], F32, name="wide", align_bytes=64)
        wv_left = keep.tile([P, 512], F32, name="wv_left")
        gained(0, gw[:])
        for k in range(2):
            stage1(k)
        gained(1, wide[:, 0:S])
        for k in range(2, 4):
            stage1(k)
        prod[0] = region(0)
        prod[1] = region(1)
        nc.vector.tensor_tensor(prod[0][:, 0:512], prod[0][:, 0:512], gw[:, 0:512], MULT)
        nc.gpsimd.tensor_tensor(prod[0][:, 512:S], prod[0][:, 512:S], gw[:, 512:S], MULT)
        nc.gpsimd.tensor_tensor(prod[1], prod[1], wide[:, 0:S], MULT)
        gained(2, gw[:])
        scatter(0, 0, 512)
        scatter(0, 512, 512)
        for k in range(4):
            weigh(nc.gpsimd, k, wv_left[:], 0, 512)
            product(k + 2, region((0, 1, 0, 4)[k]))
            scatter(k + 1, 0, S)
            wv_right = region((1, 0, 4, 0)[k])[:, 0:512]
            weigh(nc.vector, k, wv_right, 512, 512)
            visb[k + 4] = load_vis(k + 4)
            if k == 1:
                g1 = x0[:, M : 3 * M].bitcast(BF16)
                for a in range(2):
                    group_w1(g1[:, 2048 * a : 2048 * a + 2048], w1_raw[a, 1])
                gained(4, gw_late)
                codes, scales = quantise("w1q_1", g1, 1024)
                for a in range(2):
                    w1q[a, 1] = (codes[:, 512 * a : 512 * a + 512], scales[:, 512 * a : 512 * a + 512])
                for kk in range(4, 8):
                    stage1(kk)
            pick(k, x0[:, M * k : M * k + 512], 0, 512, wv_left[:])
            pick(k, x0[:, M * k + 512 : M * k + M], 512, 512, wv_right)
            if k < 3:
                page[5 + k] = load_page(5 + k)
        g3 = hbuf[0][:, 2 * S : 4 * S].bitcast(BF16)
        for u in range(2):
            weave(nc.scalar.copy, g3[:, 2048 * u : 2048 * u + 2048], w3_raw[u][:], 512)
        product(6, region(0))
        scatter(5, 0, S)
        last_prod = keep.tile([P, S], F32, name="last_prod")
        product(7, last_prod[:])
        wv = {4: region(6), 5: region(7), 6: region(0), 7: last_prod[:]}
        weigh(nc.gpsimd, 4, wv[4], 0, M)
        weigh(nc.gpsimd, 5, wv[5], 0, M)
        x0v = x0[:].rearrange("p (j m) -> p j m", j=4)
        for u in range(2):
            weave(nc.scalar.copy, wide[:, M * u : M * u + M].bitcast(BF16), x0v[:, :, 512 * u : 512 * u + 512], 512)
        scatter(6, 0, S)
        weigh(nc.gpsimd, 6, wv[6], 0, M)
        scatter(7, 0, S)
        weigh(nc.vector, 7, wv[7], 0, M)
        codes, scales = quantise("w3q", g3, 1024, tag="vis1")
        w3q = [(codes[:, 512 * u : 512 * u + 512], scales[:, 512 * u : 512 * u + 512]) for u in range(2)]
        z0 = quantise("z0", wide[:].bitcast(BF16), 1024, tag="vis2")

        stage = big("stage", "big2", F32)
        out_rows = out.rearrange("(nb p) m -> p nb m", p=P)
        starts = [sum(TAIL[:u]) for u in range(len(TAIL))]
        accs = []
        nb0 = 0
        for u, w in enumerate(TAIL):
            per = 512 // w
            banks = [bank(nb0 + v, "o%d_%d" % (u, v)) for v in range(4 // per)]
            nb0 = nb0 + 4 // per
            accs.append(banks)

        def last(u, b, codes, scales, c0):
            w = TAIL[u]
            per = 512 // w
            for nb in range(4):
                wc, ws = w3q[b]
                nc.tensor.matmul_mx(
                    out=accs[u][nb // per][:, (nb % per) * w : (nb % per + 1) * w],
                    lhsT=wc[:, 128 * nb : 128 * nb + 128].bitcast(FP8X4),
                    lhsT_scale=ws[:, 128 * nb : 128 * nb + 128],
                    rhs=codes[:, c0 : c0 + w].bitcast(FP8X4),
                    rhs_scale=scales[:, c0 : c0 + w],
                    start=(b == 0 and nb % per == 0),
                    stop=(b == 1 and nb % per == per - 1),
                )

        for u, w in enumerate(TAIL):
            last(u, 0, z0[0], z0[1], starts[u])

        xp = {}

        def picks(u):
            m0, w = starts[u], TAIL[u]
            if u < 2:
                xp[u] = wide[:, 4 * m0 : 4 * m0 + 4 * w].rearrange("p (j m) -> p j m", j=4)
            else:
                xp[u] = hbuf[0][:, 4 * m0 : 4 * m0 + 4 * w].rearrange("p (j m) -> p j m", j=4)
            for i in range(4):
                pick(4 + i, xp[u][:, i, :], m0, w, wv[4 + i][:, m0 : m0 + w])

        def woven(u):
            w = TAIL[u]
            eng = nc.vector.tensor_copy if u == len(TAIL) - 1 else nc.scalar.copy
            if u + 2 < len(TAIL):
                g = hbuf[0][:, 4 * starts[u + 2] : 4 * starts[u + 2] + 2 * w].bitcast(BF16)
            else:
                g = grouped_tile("g_z1_%d" % u)
            return weave(eng, g, xp[u], w)

        def finish(u, g):
            m0, w = starts[u], TAIL[u]
            codes, scales = quantise("z1_%d" % u, g, w)
            last(u, 1, codes, scales, 0)
            for v, acc in enumerate(accs[u]):
                eng = nc.vector.tensor_copy if u >= len(TAIL) - 2 else nc.scalar.copy
                eng(out=stage[:, 4 * m0 + 512 * v : 4 * m0 + 512 * v + 512], in_=acc[:])
            nc.sync.dma_start(
                out=out_rows[:, :, m0 : m0 + w],
                in_=stage[:, 4 * m0 : 4 * m0 + 4 * w].rearrange("p (nb m) -> p nb m", nb=4),
            )

        picks(0)
        g_prev = woven(0)
        for u in range(1, len(TAIL)):
            picks(u)
            g_next = woven(u)
            finish(u - 1, g_prev)
            g_prev = g_next
        finish(len(TAIL) - 1, g_prev)
